import numpy as np
import ml_dtypes


def mxq(x, axis, fmt="e4m3"):
    dtype, down = {"e4m3": (ml_dtypes.float8_e4m3fn, 7), "e5m2": (ml_dtypes.float8_e5m2, 14)}[fmt]
    v = np.moveaxis(np.asarray(x, np.float32).astype(ml_dtypes.bfloat16).astype(np.float64), axis, -1)
    blocks = v.reshape(v.shape[:-1] + (-1, 32))
    amax = np.abs(blocks).max(-1, keepdims=True)
    byte = np.maximum(np.where(amax > 0, np.frexp(amax)[1] - 1 + 127, 0) - down, 1)
    scale = np.exp2(byte - 127.0)
    codes = (blocks / scale).astype(np.float32).astype(dtype).astype(np.float64)
    return np.moveaxis((codes * scale).reshape(v.shape), -1, axis)


WIDE = False


def mx_kscale(k):
    if not WIDE:
        return np.ones(k)
    levels = np.array([24, -24, 12, -12, 0])
    if k % 512:
        return np.exp2(np.random.permutation(np.resize(levels, k // 32))).repeat(32)
    a = np.empty((k // 512, 16))
    for p in range(k // 512):
        a[p, :8] = np.random.permutation(np.resize(levels, 8))
        for g in range(8):
            far = levels[np.abs(levels - a[p, g]) >= 10]
            a[p, g + 8] = far[np.random.randint(len(far))]
    return np.exp2(a.ravel()).repeat(32)


def f64(x):
    return np.asarray(x).astype(np.float64)


def striped8(idx):
    return np.concatenate([v.reshape(-1, 16).T for v in idx]).astype(np.uint16)


def unstriped8(offs):
    return np.stack([offs[16 * g:16 * g + 16].T.reshape(-1) for g in range(8)]).astype(np.int64)


K, L, N, T, J = 1024, 512, 512, 2048, 1024


def setup_inputs():
    n = np.random.standard_normal
    s = mx_kscale(K)[:, None]
    s2 = mx_kscale(L)[:, None]
    return {
        "xT": (n((K, T)) * s).astype(np.float32),
        "wgt": np.repeat(np.random.uniform(0.5, 2.0, (8, J)), 16, axis=0).astype(np.float32),
        "wt": (n((K, N)) / np.sqrt(K) / s).astype(np.float32),
        "c": (n((L, J)) * s2).astype(np.float32),
        "wx": (n((L, N)) / np.sqrt(L) / s2).astype(np.float32),
        "b": (0.3 * n(N)).astype(np.float32),
        "wgo": np.repeat(np.random.uniform(0.5, 2.0, (8, J)), 16, axis=0).astype(np.float32),
        "offs": striped8(np.stack([np.random.permutation(T)[:J] for _ in range(8)])),
        "offs2": striped8(np.stack([np.random.permutation(T)[:J] for _ in range(8)])),
    }


def reference(xT, wgt, wt, c, wx, b, wgo, offs, offs2):
    idx = unstriped8(offs)
    idx2 = unstriped8(offs2)
    rows = np.arange(K)
    xg = f64(wgt)[rows // 4 % 128] * f64(xT)[rows[:, None], idx[rows % 512 // 64]]
    xT_ = mxq(xg, 0, "e4m3")
    wt_q_ = mxq(f64(wt), 0, "e4m3")
    wt_r_ = mxq(f64(wt) - wt_q_, 0, "e4m3")
    c_ = mxq(f64(c), 0, "e4m3")
    wx_ = mxq(f64(wx), 0, "e4m3")
    y = wt_q_.T @ xT_ + wt_r_.T @ xT_ + wx_.T @ c_
    out = np.zeros((N, T))
    rows = np.arange(N)
    out[rows[:, None], idx2[rows % 128 // 16]] = f64(wgo)[rows % 128] * (y + f64(b)[:, None])
    return out

@@ -1,0 +1,246 @@
+from contextlib import ExitStack
+
+import concourse.mybir as mybir
+from concourse.masks import make_identity
+
+K, L, N, T, J = 1024, 512, 512, 2048, 1024
+FLOPS = 3221225472
+
+F32 = mybir.dt.float32
+BF16 = mybir.dt.bfloat16
+U32 = mybir.dt.uint32
+I32 = mybir.dt.int32
+U16 = mybir.dt.uint16
+U8 = mybir.dt.uint8
+FP8X4 = mybir.dt.float8_e4m3fn_x4
+ALU = mybir.AluOpType
+ACT = mybir.ActivationFunctionType
+
+P = 128
+PACK = 4
+K_PASS = P * PACK
+PASSES = K // K_PASS
+N_TILES = N // P
+LIST_ROWS = 16
+CHUNKS = ((0, 128), (128, 128), (256, 256), (512, 512))
+
+
+def by_lines_src(ap):
+    return ap.rearrange("p t (c i) -> p c t i", i=4)
+
+
+def by_lines_dst(ap):
+    return ap.rearrange("p (c i) t -> p c t i", i=4)
+
+
+def tile_list_tier_scatb_kernel(tc, xT, wgt, wt, c, wx, b, wgo, offs, offs2, out):
+    nc = tc.nc
+    with ExitStack() as ctx:
+        lists = ctx.enter_context(tc.tile_pool(name="lists", bufs=1))
+        keep = ctx.enter_context(tc.tile_pool(name="keep", bufs=1))
+        raw = ctx.enter_context(tc.tile_pool(name="raw", bufs=9))
+        stage = ctx.enter_context(tc.tile_pool(name="stage", bufs=6))
+        wide = ctx.enter_context(tc.tile_pool(name="wide", bufs=3))
+        ybuf = ctx.enter_context(tc.tile_pool(name="ybuf", bufs=4))
+        negs = ctx.enter_context(tc.tile_pool(name="negs", bufs=2))
+        turns = ctx.enter_context(tc.tile_pool(name="turns", bufs=4))
+        psum_res = ctx.enter_context(tc.psum_pool(name="psum_res", bufs=4))
+        psum_acc = ctx.enter_context(tc.psum_pool(name="psum_acc", bufs=4))
+
+        def quantised(name, width):
+            codes = keep.tile([P, width], U32, name=name + "_codes", align_bytes=64)
+            scales = keep.tile([P, width], U8, name=name + "_scales", align_bytes=64)
+            return codes, scales
+
+        def staged(width):
+            if width > 256:
+                return wide.tile([P, width, PACK], BF16, name="wide_bf", tag="wide_bf", align_bytes=64)
+            return stage.tile([P, width, PACK], BF16, name="stage_bf", tag="stage_bf", align_bytes=64)
+
+        def quantise(q, cols, grouped):
+            nc.vector.quantize_mx(
+                out=q[0][:, cols].bitcast(FP8X4), scales=q[1][:, cols], in_=grouped[:].rearrange("p w t -> p (w t)")
+            )
+
+        def mm(acc, lhs, lhs_cols, rhs, rhs_cols, start, stop):
+            nc.tensor.matmul_mx(
+                out=acc,
+                lhsT=lhs[0][:, lhs_cols].bitcast(FP8X4),
+                lhsT_scale=lhs[1][:, lhs_cols],
+                rhs=rhs[0][:, rhs_cols].bitcast(FP8X4),
+                rhs_scale=rhs[1][:, rhs_cols],
+                start=start,
+                stop=stop,
+            )
+
+        def load_rows(rows, width):
+            t = raw.tile([P, PACK, width], F32, name="raw_rows", tag="raw")
+            nc.sync.dma_start(out=t[:], in_=rows.rearrange("(p t) w -> p t w", t=PACK))
+            return t
+
+        def load_plane(a, t):
+            plane = raw.tile([P, T], F32, name="raw_plane", tag="raw")
+            nc.sync.dma_start(
+                out=plane[:], in_=xT[a * K_PASS : (a + 1) * K_PASS, :].rearrange("(p t) w -> p t w", t=PACK)[:, t, :]
+            )
+            return plane
+
+        def round_and_quantise(q, q0, rows, r0, width):
+            grouped = staged(width)
+            for s in range(0, width, 256):
+                e = min(s + 256, width)
+                nc.scalar.copy(out=by_lines_dst(grouped[:, s:e, :]), in_=by_lines_src(rows[:, :, r0 + s : r0 + e]))
+            quantise(q, slice(q0, q0 + width), grouped)
+
+        offs_sb = lists.tile([P, J // LIST_ROWS], U16, name="offs_sb")
+        offs2_sb = lists.tile([P, J // LIST_ROWS], U16, name="offs2_sb")
+        nc.sync.dma_start(offs_sb[:], offs)
+        bias = keep.tile([P, N_TILES], F32, name="bias")
+        with nc.allow_non_contiguous_dma(reason="bias: one value a partition"):
+            nc.scalar.dma_start(out=bias[:], in_=b.rearrange("(m p) -> p m", p=P))
+
+        eye = keep.tile([P, P], F32, name="eye")
+        make_identity(nc, eye[:])
+        eye_bf = staged(K_PASS)
+        nc.vector.memset(eye_bf[:].rearrange("p w t -> p (w t)").bitcast(I32), 0)
+        for t in range(PACK):
+            nc.scalar.copy(out=eye_bf[:, t * P : (t + 1) * P, t], in_=eye[:])
+        eye_q = quantised("eye", K_PASS)
+        quantise(eye_q, slice(0, K_PASS), eye_bf)
+
+        pages = []
+        for m in range(N_TILES):
+            page = keep.tile([P, T], F32, name="page%d" % m)
+            nc.vector.memset(page[:], 0.0)
+            pages.append(page)
+
+        wgt_sb = keep.tile([P, J], F32, name="wgt_sb")
+        wgo_sb = keep.tile([P, J], F32, name="wgo_sb")
+        wq = [quantised("wq%d" % a, N) for a in range(PASSES)]
+        wr = [quantised("wr%d" % a, N) for a in range(PASSES)]
+        wxq = quantised("wxq", N)
+        xq = [quantised("xq%d" % a, J) for a in range(PASSES)]
+        cq = quantised("cq", J)
+
+        def first_tier(a, rows):
+            for h in range(0, N, 256):
+                round_and_quantise(wq[a], h, rows, h, 256)
+
+        def second_tier(a, rows):
+            for h in range(0, N, 256):
+                left = staged(256)
+                for m0 in range(h, h + 256, P):
+                    back = psum_res.tile([P, PACK, P], F32, name="back", tag="res")
+                    for t in range(PACK):
+                        mm(back[:, t, :], eye_q, slice(t * P, (t + 1) * P), wq[a], slice(m0, m0 + P), True, True)
+                    nc.vector.tensor_tensor(
+                        out=by_lines_dst(left[:, m0 - h : m0 - h + P, :]),
+                        in0=by_lines_src(rows[:, :, m0 : m0 + P]),
+                        in1=by_lines_src(back[:]),
+                        op=ALU.subtract,
+                    )
+                quantise(wr[a], slice(h, h + 256), left)
+
+        def second_tier_on_tensor(a, rows):
+            for h in range(0, N, 256):
+                neg = negs.tile([P, PACK, 256], F32, name="neg", tag="neg")
+                for u in range(2):
+                    back = psum_res.tile([P, 2, 256], F32, name="back2", tag="res")
+                    for e in range(2):
+                        t = 2 * u + e
+                        mm(back[:, e, :], eye_q, slice(t * P, (t + 1) * P), wq[a], slice(h, h + 256), True, True)
+                    nc.scalar.activation(out=neg[:, 2 * u : 2 * u + 2, :], in_=back[:], func=ACT.Copy, scale=-1.0)
+                turned = []
+                for s in range(0, 256, P):
+                    diff = psum_res.tile([P, PACK, P], F32, name="diff", tag="res")
+                    for t in range(PACK):
+                        nc.tensor.matmul(
+                            diff[:, t, :], lhsT=rows[:, t, h + s : h + s + P], rhs=eye[:],
+                            start=True, stop=False, is_transpose=True,
+                        )
+                        nc.tensor.matmul(
+                            diff[:, t, :], lhsT=neg[:, t, s : s + P], rhs=eye[:],
+                            start=False, stop=True, is_transpose=True,
+                        )
+                    pairs = turns.tile([P, 2, P, 2], BF16, name="pairs", tag="pairs")
+                    nc.scalar.copy(out=pairs[:], in_=diff[:].rearrange("n (u e) p -> n u p e", e=2))
+                    turned.append(pairs)
+                words = psum_res.tile([P, 2, 2, P], F32, name="words", tag="res")
+                for s, pairs in enumerate(turned):
+                    as_words = pairs[:].rearrange("n u p e -> n (u p e)").bitcast(F32)
+                    for u in range(2):
+                        nc.tensor.transpose(words[:, s, u, :], as_words[:, u * P : (u + 1) * P], eye[:])
+                left = staged(256)
+                nc.scalar.copy(
+                    out=left[:].rearrange("p w t -> p (w t)").bitcast(F32).rearrange("p (s n u) -> p s n u", s=2, u=2),
+                    in_=words[:].rearrange("p s u n -> p s n u"),
+                )
+                quantise(wr[a], slice(h, h + 256), left)
+
+        def gather(dst, plane, j0, width):
+            nc.vector.tensor_tensor(
+                dst,
+                plane[:].indirect(offs_sb[:, j0 // LIST_ROWS : (j0 + width) // LIST_ROWS]),
+                wgt_sb[:, j0 : j0 + width],
+                ALU.mult,
+            )
+
+        picked0 = keep.tile([P, PACK, J], F32, name="picked0")
+        picked1 = [keep.tile([P, PACK, w], F32, name="picked1_%d" % j0) for j0, w in CHUNKS]
+
+        def gather_plane(a, t):
+            plane = load_plane(a, t)
+            if a == 0:
+                gather(picked0[:, t, :], plane, 0, J)
+            else:
+                for (j0, w), dst in zip(CHUNKS, picked1):
+                    gather(dst[:, t, :], plane, j0, w)
+
+        wt0 = load_rows(wt[0:K_PASS, :], N)
+        nc.sync.dma_start(out=wgt_sb[:], in_=wgt)
+        first_tier(0, wt0)
+        second_tier(0, wt0)
+        gather_plane(0, 0)
+        wt1 = load_rows(wt[K_PASS:K, :], N)
+        first_tier(1, wt1)
+        gather_plane(0, 1)
+        second_tier_on_tensor(1, wt1)
+        gather_plane(0, 2)
+        gather_plane(0, 3)
+        wx_rows = load_rows(wx, N)
+        gather_plane(1, 0)
+        for h in range(0, J, 512):
+            round_and_quantise(xq[0], h, picked0, h, 512)
+        round_and_quantise(wxq, 0, wx_rows, 0, N)
+        for t in range(1, PACK):
+            gather_plane(1, t)
+
+        c_rows = []
+        for i, (j0, w) in enumerate(CHUNKS):
+            c_rows.append(load_rows(c[:, j0 : j0 + w], w))
+            if i == 0:
+                nc.sync.dma_start(out=wgo_sb[:, 0:256], in_=wgo[:, 0:256])
+                nc.sync.dma_start(offs2_sb[:], offs2)
+            if i == 2:
+                nc.sync.dma_start(out=wgo_sb[:, 256:J], in_=wgo[:, 256:J])
+
+        for i, (j0, w) in enumerate(CHUNKS):
+            cols = slice(j0, j0 + w)
+            round_and_quantise(xq[1], j0, picked1[i], 0, w)
+            round_and_quantise(cq, j0, c_rows[i], 0, w)
+            for m in range(N_TILES):
+                rows = slice(m * P, (m + 1) * P)
+                acc = psum_acc.tile([P, w], F32, name="acc", tag="acc")
+                terms = [(wq[0], xq[0]), (wr[0], xq[0]), (wq[1], xq[1]), (wr[1], xq[1]), (wxq, cq)]
+                for n, (lhs, rhs) in enumerate(terms):
+                    mm(acc[:], lhs, rows, rhs, cols, n == 0, n == len(terms) - 1)
+                y = ybuf.tile([P, w], F32, name="y", tag="y")
+                nc.scalar.activation(out=y[:], in_=acc[:], func=ACT.Identity, bias=bias[:, m : m + 1], scale=1.0)
+                nc.vector.tensor_tensor(
+                    pages[m][:].indirect(offs2_sb[:, j0 // LIST_ROWS : (j0 + w) // LIST_ROWS]),
+                    y[:],
+                    wgo_sb[:, cols],
+                    ALU.mult,
+                )
+                if i == len(CHUNKS) - 1:
+                    nc.sync.dma_start(out=out[rows, :], in_=pages[m][:])

@@ -22,7 +22,8 @@ K_PASS = P * PACK
 PASSES = K // K_PASS
 N_TILES = N // P
 LIST_ROWS = 16
-CHUNKS = ((0, 128), (128, 128), (256, 256), (512, 512))
+HALF = J // 2
+PIECE = 256
 
 
 def by_lines_src(ap):
@@ -39,208 +40,232 @@ def tile_list_tier_scatb_kernel(tc, xT, wgt, wt, c, wx, b, wgo, offs, offs2, out
         lists = ctx.enter_context(tc.tile_pool(name="lists", bufs=1))
         keep = ctx.enter_context(tc.tile_pool(name="keep", bufs=1))
         raw = ctx.enter_context(tc.tile_pool(name="raw", bufs=9))
-        stage = ctx.enter_context(tc.tile_pool(name="stage", bufs=6))
-        wide = ctx.enter_context(tc.tile_pool(name="wide", bufs=3))
-        ybuf = ctx.enter_context(tc.tile_pool(name="ybuf", bufs=4))
+        stage = ctx.enter_context(tc.tile_pool(name="stage", bufs=8))
         negs = ctx.enter_context(tc.tile_pool(name="negs", bufs=2))
         turns = ctx.enter_context(tc.tile_pool(name="turns", bufs=4))
-        psum_res = ctx.enter_context(tc.psum_pool(name="psum_res", bufs=4))
-        psum_acc = ctx.enter_context(tc.psum_pool(name="psum_acc", bufs=4))
+        ybuf = ctx.enter_context(tc.tile_pool(name="ybuf", bufs=4))
+        psum_res = ctx.enter_context(tc.psum_pool(name="psum_res", bufs=5))
+        psum_acc = ctx.enter_context(tc.psum_pool(name="psum_acc", bufs=3))
 
         def quantised(name, width):
             codes = keep.tile([P, width], U32, name=name + "_codes", align_bytes=64)
             scales = keep.tile([P, width], U8, name=name + "_scales", align_bytes=64)
             return codes, scales
 
-        def staged(width):
-            if width > 256:
-                return wide.tile([P, width, PACK], BF16, name="wide_bf", tag="wide_bf", align_bytes=64)
-            return stage.tile([P, width, PACK], BF16, name="stage_bf", tag="stage_bf", align_bytes=64)
+        def staged():
+            return stage.tile([P, PIECE, PACK], BF16, name="staged", tag="staged", align_bytes=64)
 
-        def quantise(q, cols, grouped):
+        def quantise(q, q0, grouped):
+            cols = slice(q0, q0 + grouped.shape[1])
             nc.vector.quantize_mx(
                 out=q[0][:, cols].bitcast(FP8X4), scales=q[1][:, cols], in_=grouped[:].rearrange("p w t -> p (w t)")
             )
 
-        def mm(acc, lhs, lhs_cols, rhs, rhs_cols, start, stop):
+        def mm(acc, lhs, lhs0, rhs, start, stop):
             nc.tensor.matmul_mx(
                 out=acc,
-                lhsT=lhs[0][:, lhs_cols].bitcast(FP8X4),
-                lhsT_scale=lhs[1][:, lhs_cols],
-                rhs=rhs[0][:, rhs_cols].bitcast(FP8X4),
-                rhs_scale=rhs[1][:, rhs_cols],
+                lhsT=lhs[0][:, lhs0 : lhs0 + P].bitcast(FP8X4),
+                lhsT_scale=lhs[1][:, lhs0 : lhs0 + P],
+                rhs=rhs[0][:].bitcast(FP8X4),
+                rhs_scale=rhs[1][:],
                 start=start,
                 stop=stop,
             )
 
-        def load_rows(rows, width):
-            t = raw.tile([P, PACK, width], F32, name="raw_rows", tag="raw")
-            nc.sync.dma_start(out=t[:], in_=rows.rearrange("(p t) w -> p t w", t=PACK))
-            return t
+        def load_rows(rows, tile):
+            nc.sync.dma_start(out=tile[:], in_=rows.rearrange("(p t) w -> p t w", t=PACK))
+            return tile
+
+        def ring_rows():
+            return raw.tile([P, PACK, HALF], F32, name="ring_rows", tag="raw")
 
         def load_plane(a, t):
-            plane = raw.tile([P, T], F32, name="raw_plane", tag="raw")
+            plane = raw.tile([P, T], F32, name="plane", tag="raw")
             nc.sync.dma_start(
                 out=plane[:], in_=xT[a * K_PASS : (a + 1) * K_PASS, :].rearrange("(p t) w -> p t w", t=PACK)[:, t, :]
             )
             return plane
 
-        def round_and_quantise(q, q0, rows, r0, width):
-            grouped = staged(width)
-            for s in range(0, width, 256):
-                e = min(s + 256, width)
-                nc.scalar.copy(out=by_lines_dst(grouped[:, s:e, :]), in_=by_lines_src(rows[:, :, r0 + s : r0 + e]))
-            quantise(q, slice(q0, q0 + width), grouped)
+        def round_and_quantise(q, q0, rows, r0, grouped):
+            nc.scalar.copy(out=by_lines_dst(grouped[:]), in_=by_lines_src(rows[:, :, r0 : r0 + grouped.shape[1]]))
+            quantise(q, q0, grouped)
 
         offs_sb = lists.tile([P, J // LIST_ROWS], U16, name="offs_sb")
         offs2_sb = lists.tile([P, J // LIST_ROWS], U16, name="offs2_sb")
         nc.sync.dma_start(offs_sb[:], offs)
         bias = keep.tile([P, N_TILES], F32, name="bias")
-        with nc.allow_non_contiguous_dma(reason="bias: one value a partition"):
-            nc.scalar.dma_start(out=bias[:], in_=b.rearrange("(m p) -> p m", p=P))
+        bias_rows = keep.tile([P, P], F32, name="bias_rows")
 
         eye = keep.tile([P, P], F32, name="eye")
         make_identity(nc, eye[:])
-        eye_bf = staged(K_PASS)
-        nc.vector.memset(eye_bf[:].rearrange("p w t -> p (w t)").bitcast(I32), 0)
-        for t in range(PACK):
-            nc.scalar.copy(out=eye_bf[:, t * P : (t + 1) * P, t], in_=eye[:])
+        nc.gpsimd.memset(bias_rows[:], 0.0)
         eye_q = quantised("eye", K_PASS)
-        quantise(eye_q, slice(0, K_PASS), eye_bf)
+        for u in range(2):
+            eye_bf = keep.tile([P, PIECE, PACK], BF16, name="eye_bf", tag="picked0_%d" % u, align_bytes=64)
+            nc.vector.memset(eye_bf[:].rearrange("p w t -> p (w t)").bitcast(I32), 0)
+            for e in range(2):
+                nc.vector.tensor_copy(out=eye_bf[:, e * P : (e + 1) * P, 2 * u + e], in_=eye[:])
+            quantise(eye_q, u * PIECE, eye_bf)
 
-        pages = []
-        for m in range(N_TILES):
-            page = keep.tile([P, T], F32, name="page%d" % m)
-            nc.vector.memset(page[:], 0.0)
-            pages.append(page)
+        pages = {}
 
-        wgt_sb = keep.tile([P, J], F32, name="wgt_sb")
-        wgo_sb = keep.tile([P, J], F32, name="wgo_sb")
-        wq = [quantised("wq%d" % a, N) for a in range(PASSES)]
-        wr = [quantised("wr%d" % a, N) for a in range(PASSES)]
-        wxq = quantised("wxq", N)
-        xq = [quantised("xq%d" % a, J) for a in range(PASSES)]
-        cq = quantised("cq", J)
+        def clear_page(m, engine, words):
+            page = keep.tile([P, T], F32, name="page", tag="page%d" % m, align_bytes=64)
+            for w0 in range(0, T, words):
+                engine.memset(page[:, w0 : w0 + words].bitcast(I32), 0)
+            pages[m] = page
 
-        def first_tier(a, rows):
-            for h in range(0, N, 256):
-                round_and_quantise(wq[a], h, rows, h, 256)
+        clear_page(0, nc.vector, T)
+        clear_page(1, nc.vector, T)
 
-        def second_tier(a, rows):
-            for h in range(0, N, 256):
-                left = staged(256)
-                for m0 in range(h, h + 256, P):
-                    back = psum_res.tile([P, PACK, P], F32, name="back", tag="res")
-                    for t in range(PACK):
-                        mm(back[:, t, :], eye_q, slice(t * P, (t + 1) * P), wq[a], slice(m0, m0 + P), True, True)
-                    nc.vector.tensor_tensor(
-                        out=by_lines_dst(left[:, m0 - h : m0 - h + P, :]),
-                        in0=by_lines_src(rows[:, :, m0 : m0 + P]),
-                        in1=by_lines_src(back[:]),
-                        op=ALU.subtract,
-                    )
-                quantise(wr[a], slice(h, h + 256), left)
+        wgt_sb = [keep.tile([P, HALF], F32, name="wgt_sb", tag="wgt%d" % h, align_bytes=64) for h in range(2)]
+        wgo_sb = [keep.tile([P, HALF], F32, name="wgo_sb", tag="wgo%d" % h) for h in range(2)]
+        wq = [[quantised("wq%d%d" % (a, s), PIECE) for s in range(2)] for a in range(PASSES)]
+        wr = [[quantised("wr%d%d" % (a, s), PIECE) for s in range(2)] for a in range(PASSES)]
+        wxq = [quantised("wxq%d" % s, PIECE) for s in range(2)]
+        xq = [[quantised("xq%d%d" % (a, h), HALF) for h in range(2)] for a in range(PASSES)]
+        cq = [quantised("cq%d" % h, HALF) for h in range(2)]
 
-        def second_tier_on_tensor(a, rows):
-            for h in range(0, N, 256):
-                neg = negs.tile([P, PACK, 256], F32, name="neg", tag="neg")
-                for u in range(2):
-                    back = psum_res.tile([P, 2, 256], F32, name="back2", tag="res")
-                    for e in range(2):
-                        t = 2 * u + e
-                        mm(back[:, e, :], eye_q, slice(t * P, (t + 1) * P), wq[a], slice(h, h + 256), True, True)
-                    nc.scalar.activation(out=neg[:, 2 * u : 2 * u + 2, :], in_=back[:], func=ACT.Copy, scale=-1.0)
-                turned = []
-                for s in range(0, 256, P):
-                    diff = psum_res.tile([P, PACK, P], F32, name="diff", tag="res")
-                    for t in range(PACK):
-                        nc.tensor.matmul(
-                            diff[:, t, :], lhsT=rows[:, t, h + s : h + s + P], rhs=eye[:],
-                            start=True, stop=False, is_transpose=True,
-                        )
-                        nc.tensor.matmul(
-                            diff[:, t, :], lhsT=neg[:, t, s : s + P], rhs=eye[:],
-                            start=False, stop=True, is_transpose=True,
-                        )
-                    pairs = turns.tile([P, 2, P, 2], BF16, name="pairs", tag="pairs")
-                    nc.scalar.copy(out=pairs[:], in_=diff[:].rearrange("n (u e) p -> n u p e", e=2))
-                    turned.append(pairs)
-                words = psum_res.tile([P, 2, 2, P], F32, name="words", tag="res")
-                for s, pairs in enumerate(turned):
-                    as_words = pairs[:].rearrange("n u p e -> n (u p e)").bitcast(F32)
-                    for u in range(2):
-                        nc.tensor.transpose(words[:, s, u, :], as_words[:, u * P : (u + 1) * P], eye[:])
-                left = staged(256)
-                nc.scalar.copy(
-                    out=left[:].rearrange("p w t -> p (w t)").bitcast(F32).rearrange("p (s n u) -> p s n u", s=2, u=2),
-                    in_=words[:].rearrange("p s u n -> p s n u"),
-                )
-                quantise(wr[a], slice(h, h + 256), left)
+        def stationary(q, rows):
+            for s in range(2):
+                round_and_quantise(q[s], 0, rows, s * PIECE, staged())
 
-        def gather(dst, plane, j0, width):
-            nc.vector.tensor_tensor(
-                dst,
-                plane[:].indirect(offs_sb[:, j0 // LIST_ROWS : (j0 + width) // LIST_ROWS]),
-                wgt_sb[:, j0 : j0 + width],
-                ALU.mult,
-            )
+        def moving(q, rows, buffers):
+            for s in range(2):
+                round_and_quantise(q, s * PIECE, rows, s * PIECE, buffers[s])
 
-        picked0 = keep.tile([P, PACK, J], F32, name="picked0")
-        picked1 = [keep.tile([P, PACK, w], F32, name="picked1_%d" % j0) for j0, w in CHUNKS]
+        def named_stage(tag, width):
+            return keep.tile([P, width, PACK], BF16, name="named_stage", tag=tag, align_bytes=64)
 
-        def gather_plane(a, t):
-            plane = load_plane(a, t)
-            if a == 0:
-                gather(picked0[:, t, :], plane, 0, J)
-            else:
-                for (j0, w), dst in zip(CHUNKS, picked1):
-                    gather(dst[:, t, :], plane, j0, w)
-
-        wt0 = load_rows(wt[0:K_PASS, :], N)
-        nc.sync.dma_start(out=wgt_sb[:], in_=wgt)
-        first_tier(0, wt0)
-        second_tier(0, wt0)
-        gather_plane(0, 0)
-        wt1 = load_rows(wt[K_PASS:K, :], N)
-        first_tier(1, wt1)
-        gather_plane(0, 1)
-        second_tier_on_tensor(1, wt1)
-        gather_plane(0, 2)
-        gather_plane(0, 3)
-        wx_rows = load_rows(wx, N)
-        gather_plane(1, 0)
-        for h in range(0, J, 512):
-            round_and_quantise(xq[0], h, picked0, h, 512)
-        round_and_quantise(wxq, 0, wx_rows, 0, N)
-        for t in range(1, PACK):
-            gather_plane(1, t)
-
-        c_rows = []
-        for i, (j0, w) in enumerate(CHUNKS):
-            c_rows.append(load_rows(c[:, j0 : j0 + w], w))
-            if i == 0:
-                nc.sync.dma_start(out=wgo_sb[:, 0:256], in_=wgo[:, 0:256])
-                nc.sync.dma_start(offs2_sb[:], offs2)
-            if i == 2:
-                nc.sync.dma_start(out=wgo_sb[:, 256:J], in_=wgo[:, 256:J])
-
-        for i, (j0, w) in enumerate(CHUNKS):
-            cols = slice(j0, j0 + w)
-            round_and_quantise(xq[1], j0, picked1[i], 0, w)
-            round_and_quantise(cq, j0, c_rows[i], 0, w)
-            for m in range(N_TILES):
-                rows = slice(m * P, (m + 1) * P)
-                acc = psum_acc.tile([P, w], F32, name="acc", tag="acc")
-                terms = [(wq[0], xq[0]), (wr[0], xq[0]), (wq[1], xq[1]), (wr[1], xq[1]), (wxq, cq)]
-                for n, (lhs, rhs) in enumerate(terms):
-                    mm(acc[:], lhs, rows, rhs, cols, n == 0, n == len(terms) - 1)
-                y = ybuf.tile([P, w], F32, name="y", tag="y")
-                nc.scalar.activation(out=y[:], in_=acc[:], func=ACT.Identity, bias=bias[:, m : m + 1], scale=1.0)
+        def second_tier_on_vector(a, s, rows, r0, left):
+            for m0 in range(0, PIECE, P):
+                back = psum_res.tile([P, PACK, P], F32, name="back", tag="res")
+                first = (wq[a][s][0][:, m0 : m0 + P], wq[a][s][1][:, m0 : m0 + P])
+                for t in range(PACK):
+                    mm(back[:, t, :], eye_q, t * P, first, True, True)
                 nc.vector.tensor_tensor(
-                    pages[m][:].indirect(offs2_sb[:, j0 // LIST_ROWS : (j0 + w) // LIST_ROWS]),
-                    y[:],
-                    wgo_sb[:, cols],
-                    ALU.mult,
+                    out=by_lines_dst(left[:, m0 : m0 + P, :]),
+                    in0=by_lines_src(rows[:, :, r0 + m0 : r0 + m0 + P]),
+                    in1=by_lines_src(back[:]),
+                    op=ALU.subtract,
                 )
-                if i == len(CHUNKS) - 1:
-                    nc.sync.dma_start(out=out[rows, :], in_=pages[m][:])
+            quantise(wr[a][s], 0, left)
+
+        def second_tier(a, s, rows, r0):
+            neg = negs.tile([P, PACK, PIECE], F32, name="neg", tag="neg")
+            for u in range(2):
+                back = psum_res.tile([P, 2, PIECE], F32, name="back", tag="res")
+                for e in range(2):
+                    mm(back[:, e, :], eye_q, (2 * u + e) * P, wq[a][s], True, True)
+                nc.scalar.activation(out=neg[:, 2 * u : 2 * u + 2, :], in_=back[:], func=ACT.Copy, scale=-1.0)
+            turned = []
+            for m0 in range(0, PIECE, P):
+                diff = psum_res.tile([P, PACK, P], F32, name="diff", tag="res")
+                for t in range(PACK):
+                    nc.tensor.matmul(
+                        diff[:, t, :], lhsT=rows[:, t, r0 + m0 : r0 + m0 + P], rhs=eye[:],
+                        start=True, stop=False, is_transpose=True,
+                    )
+                    nc.tensor.matmul(
+                        diff[:, t, :], lhsT=neg[:, t, m0 : m0 + P], rhs=eye[:],
+                        start=False, stop=True, is_transpose=True,
+                    )
+                pairs = turns.tile([P, 2, P, 2], BF16, name="pairs", tag="pairs")
+                nc.scalar.copy(out=pairs[:], in_=diff[:].rearrange("n (u e) p -> n u p e", e=2))
+                turned.append(pairs)
+            words = psum_res.tile([P, 2, 2, P], F32, name="words", tag="res")
+            for i, pairs in enumerate(turned):
+                as_words = pairs[:].rearrange("n u p e -> n (u p e)").bitcast(F32)
+                for u in range(2):
+                    nc.tensor.transpose(words[:, i, u, :], as_words[:, u * P : (u + 1) * P], eye[:])
+            left = staged()
+            nc.scalar.copy(
+                out=left[:].rearrange("p w t -> p (w t)").bitcast(F32).rearrange("p (i n u) -> p i n u", i=2, u=2),
+                in_=words[:].rearrange("p i u n -> p i n u"),
+            )
+            quantise(wr[a][s], 0, left)
+
+        def list_half(sb, h):
+            return sb[:, h * HALF // LIST_ROWS : (h + 1) * HALF // LIST_ROWS]
+
+        def gather(dst, plane, h):
+            nc.vector.tensor_tensor(dst, plane[:].indirect(list_half(offs_sb, h)), wgt_sb[h][:], ALU.mult)
+
+        def finish(h, m, y):
+            s, m0 = divmod(m * P, PIECE)
+            acc = psum_acc.tile([P, HALF], F32, name="acc", tag="acc")
+            terms = [(wq[0], xq[0][h]), (wr[0], xq[0][h]), (wq[1], xq[1][h]), (wr[1], xq[1][h]), (wxq, cq[h])]
+            for n, (lhs, rhs) in enumerate(terms):
+                mm(acc[:], lhs[s], m0, rhs, n == 0, n == len(terms) - 1)
+            nc.scalar.activation(out=y[:], in_=acc[:], func=ACT.Identity, bias=bias[:, m : m + 1], scale=1.0)
+            nc.vector.tensor_tensor(pages[m][:].indirect(list_half(offs2_sb, h)), y[:], wgo_sb[h][:], ALU.mult)
+
+        def ring_y():
+            return ybuf.tile([P, HALF], F32, name="y", tag="y")
+
+        picked0 = [keep.tile([P, PACK, HALF], F32, name="picked0", tag="picked0_%d" % h, align_bytes=64) for h in range(2)]
+        early = keep.tile([P, PACK, HALF], F32, name="early")
+        planes = []
+
+        def gather_first_pass(t, plane):
+            for h in range(2):
+                gather(picked0[h][:, t, :], plane, h)
+
+        def gather_early(t):
+            planes.append(load_plane(1, t))
+            gather(early[:, t, :], planes[t], 0)
+
+        wt0 = load_rows(wt[0:K_PASS, :], ring_rows())
+        nc.sync.dma_start(out=wgt_sb[0][:], in_=wgt[:, 0:HALF])
+        plane = load_plane(0, 0)
+        nc.sync.dma_start(out=wgt_sb[1][:], in_=wgt[:, HALF:J])
+        wt1 = load_rows(wt[K_PASS:K, :], ring_rows())
+        stationary(wq[0], wt0)
+        for s in range(2):
+            second_tier_on_vector(0, s, wt0, s * PIECE, staged())
+        gather_first_pass(0, plane)
+        for s in range(2):
+            round_and_quantise(wq[1][s], 0, wt1, s * PIECE, named_stage("page%d" % (2 + s), PIECE))
+            clear_page(2 + s, nc.gpsimd, HALF)
+        for s in range(2):
+            second_tier(1, s, wt1, s * PIECE)
+        for t in range(1, PACK):
+            gather_first_pass(t, load_plane(0, t))
+        nc.sync.dma_start(out=bias_rows[0:N_TILES, :], in_=b.rearrange("(m p) -> m p", p=P))
+        bias_turned = psum_res.tile([P, P], F32, name="bias_turned", tag="res")
+        nc.tensor.transpose(bias_turned[:], bias_rows[:], eye[:])
+        nc.scalar.copy(out=bias[:], in_=bias_turned[:, 0:N_TILES])
+        round_and_quantise(xq[0][0], 0, picked0[0], 0, named_stage("wide", HALF))
+
+        gather_early(0)
+        gather_early(1)
+        wx_rows = load_rows(wx, ring_rows())
+        stationary(wxq, wx_rows)
+        gather_early(2)
+        gather_early(3)
+        c_early = load_rows(c[:, 0:HALF], ring_rows())
+        nc.sync.dma_start(out=wgo_sb[0][:], in_=wgo[:, 0:HALF])
+        nc.sync.dma_start(offs2_sb[:], offs2)
+        c_late = load_rows(c[:, HALF:J], keep.tile([P, PACK, HALF], F32, name="c_late", tag="c_late"))
+        nc.sync.dma_start(out=wgo_sb[1][:], in_=wgo[:, HALF:J])
+
+        late_row = keep.tile([P, PACK * HALF], F32, name="late_row", tag="wgt0", align_bytes=64)
+        late = late_row[:].rearrange("p (t w) -> p t w", t=PACK)
+
+        def borrowed(t):
+            return late_row[:, t * HALF : (t + 1) * HALF].bitcast(BF16).rearrange("p (w t) -> p w t", t=PACK)
+
+        moving(xq[1][0], early, [staged(), borrowed(3)])
+        moving(cq[0], c_early, [named_stage("hold", PIECE), borrowed(2)])
+        for t in (0, 1, 3, 2):
+            gather(late_row[:, t * HALF : (t + 1) * HALF], planes[t], 1)
+        finish(0, 0, ring_y())
+        finish(0, 1, ring_y())
+        round_and_quantise(xq[0][1], 0, picked0[1], 0, named_stage("hold", HALF))
+        round_and_quantise(xq[1][1], 0, late, 0, named_stage("wide", HALF))
+        round_and_quantise(cq[1], 0, c_late, 0, named_stage("hold", HALF))
+        finish(0, 2, keep.tile([P, HALF], F32, name="y_after_late", tag="wgt0", align_bytes=64))
+        finish(0, 3, keep.tile([P, HALF], F32, name="y_after_c", tag="c_late"))
+        for m in range(N_TILES):
+            finish(1, m, ring_y())
+            nc.sync.dma_start(out=out[m * P : (m + 1) * P, :], in_=pages[m][:])

from contextlib import ExitStack

import concourse.mybir as mybir
from concourse.masks import make_identity

K, L, N, T, J = 1024, 512, 512, 2048, 1024
FLOPS = 3221225472

F32 = mybir.dt.float32
BF16 = mybir.dt.bfloat16
U32 = mybir.dt.uint32
I32 = mybir.dt.int32
U16 = mybir.dt.uint16
U8 = mybir.dt.uint8
FP8X4 = mybir.dt.float8_e4m3fn_x4
ALU = mybir.AluOpType
ACT = mybir.ActivationFunctionType

P = 128
PACK = 4
K_PASS = P * PACK
PASSES = K // K_PASS
N_TILES = N // P
LIST_ROWS = 16
HALF = J // 2
PIECE = 256


def by_lines_src(ap):
    return ap.rearrange("p t (c i) -> p c t i", i=4)


def by_lines_dst(ap):
    return ap.rearrange("p (c i) t -> p c t i", i=4)


def tile_list_tier_scatb_kernel(tc, xT, wgt, wt, c, wx, b, wgo, offs, offs2, out):
    nc = tc.nc
    with ExitStack() as ctx:
        lists = ctx.enter_context(tc.tile_pool(name="lists", bufs=1))
        keep = ctx.enter_context(tc.tile_pool(name="keep", bufs=1))
        raw = ctx.enter_context(tc.tile_pool(name="raw", bufs=9))
        stage = ctx.enter_context(tc.tile_pool(name="stage", bufs=8))
        negs = ctx.enter_context(tc.tile_pool(name="negs", bufs=2))
        turns = ctx.enter_context(tc.tile_pool(name="turns", bufs=4))
        ybuf = ctx.enter_context(tc.tile_pool(name="ybuf", bufs=4))
        psum_res = ctx.enter_context(tc.psum_pool(name="psum_res", bufs=5))
        psum_acc = ctx.enter_context(tc.psum_pool(name="psum_acc", bufs=3))

        def quantised(name, width):
            codes = keep.tile([P, width], U32, name=name + "_codes", align_bytes=64)
            scales = keep.tile([P, width], U8, name=name + "_scales", align_bytes=64)
            return codes, scales

        def staged():
            return stage.tile([P, PIECE, PACK], BF16, name="staged", tag="staged", align_bytes=64)

        def quantise(q, q0, grouped):
            cols = slice(q0, q0 + grouped.shape[1])
            nc.vector.quantize_mx(
                out=q[0][:, cols].bitcast(FP8X4), scales=q[1][:, cols], in_=grouped[:].rearrange("p w t -> p (w t)")
            )

        def mm(acc, lhs, lhs0, rhs, start, stop):
            nc.tensor.matmul_mx(
                out=acc,
                lhsT=lhs[0][:, lhs0 : lhs0 + P].bitcast(FP8X4),
                lhsT_scale=lhs[1][:, lhs0 : lhs0 + P],
                rhs=rhs[0][:].bitcast(FP8X4),
                rhs_scale=rhs[1][:],
                start=start,
                stop=stop,
            )

        def load_rows(rows, tile):
            nc.sync.dma_start(out=tile[:], in_=rows.rearrange("(p t) w -> p t w", t=PACK))
            return tile

        def ring_rows():
            return raw.tile([P, PACK, HALF], F32, name="ring_rows", tag="raw")

        def load_plane(a, t):
            plane = raw.tile([P, T], F32, name="plane", tag="raw")
            nc.sync.dma_start(
                out=plane[:], in_=xT[a * K_PASS : (a + 1) * K_PASS, :].rearrange("(p t) w -> p t w", t=PACK)[:, t, :]
            )
            return plane

        def round_and_quantise(q, q0, rows, r0, grouped):
            nc.scalar.copy(out=by_lines_dst(grouped[:]), in_=by_lines_src(rows[:, :, r0 : r0 + grouped.shape[1]]))
            quantise(q, q0, grouped)

        offs_sb = lists.tile([P, J // LIST_ROWS], U16, name="offs_sb")
        offs2_sb = lists.tile([P, J // LIST_ROWS], U16, name="offs2_sb")
        nc.sync.dma_start(offs_sb[:], offs)
        bias = keep.tile([P, N_TILES], F32, name="bias")
        bias_rows = keep.tile([P, P], F32, name="bias_rows")

        eye = keep.tile([P, P], F32, name="eye")
        make_identity(nc, eye[:])
        nc.gpsimd.memset(bias_rows[:], 0.0)
        eye_q = quantised("eye", K_PASS)
        for u in range(2):
            eye_bf = keep.tile([P, PIECE, PACK], BF16, name="eye_bf", tag="picked0_%d" % u, align_bytes=64)
            nc.vector.memset(eye_bf[:].rearrange("p w t -> p (w t)").bitcast(I32), 0)
            for e in range(2):
                nc.vector.tensor_copy(out=eye_bf[:, e * P : (e + 1) * P, 2 * u + e], in_=eye[:])
            quantise(eye_q, u * PIECE, eye_bf)

        pages = {}

        def clear_page(m, engine, words):
            page = keep.tile([P, T], F32, name="page", tag="page%d" % m, align_bytes=64)
            for w0 in range(0, T, words):
                engine.memset(page[:, w0 : w0 + words].bitcast(I32), 0)
            pages[m] = page

        clear_page(0, nc.vector, T)
        clear_page(1, nc.vector, T)

        wgt_sb = [keep.tile([P, HALF], F32, name="wgt_sb", tag="wgt%d" % h, align_bytes=64) for h in range(2)]
        wgo_sb = [keep.tile([P, HALF], F32, name="wgo_sb", tag="wgo%d" % h) for h in range(2)]
        wq = [[quantised("wq%d%d" % (a, s), PIECE) for s in range(2)] for a in range(PASSES)]
        wr = [[quantised("wr%d%d" % (a, s), PIECE) for s in range(2)] for a in range(PASSES)]
        wxq = [quantised("wxq%d" % s, PIECE) for s in range(2)]
        xq = [[quantised("xq%d%d" % (a, h), HALF) for h in range(2)] for a in range(PASSES)]
        cq = [quantised("cq%d" % h, HALF) for h in range(2)]

        def stationary(q, rows):
            for s in range(2):
                round_and_quantise(q[s], 0, rows, s * PIECE, staged())

        def moving(q, rows, buffers):
            for s in range(2):
                round_and_quantise(q, s * PIECE, rows, s * PIECE, buffers[s])

        def named_stage(tag, width):
            return keep.tile([P, width, PACK], BF16, name="named_stage", tag=tag, align_bytes=64)

        def second_tier_on_vector(a, s, rows, r0, left):
            for m0 in range(0, PIECE, P):
                back = psum_res.tile([P, PACK, P], F32, name="back", tag="res")
                first = (wq[a][s][0][:, m0 : m0 + P], wq[a][s][1][:, m0 : m0 + P])
                for t in range(PACK):
                    mm(back[:, t, :], eye_q, t * P, first, True, True)
                nc.vector.tensor_tensor(
                    out=by_lines_dst(left[:, m0 : m0 + P, :]),
                    in0=by_lines_src(rows[:, :, r0 + m0 : r0 + m0 + P]),
                    in1=by_lines_src(back[:]),
                    op=ALU.subtract,
                )
            quantise(wr[a][s], 0, left)

        def second_tier(a, s, rows, r0):
            neg = negs.tile([P, PACK, PIECE], F32, name="neg", tag="neg")
            for u in range(2):
                back = psum_res.tile([P, 2, PIECE], F32, name="back", tag="res")
                for e in range(2):
                    mm(back[:, e, :], eye_q, (2 * u + e) * P, wq[a][s], True, True)
                nc.scalar.activation(out=neg[:, 2 * u : 2 * u + 2, :], in_=back[:], func=ACT.Copy, scale=-1.0)
            turned = []
            for m0 in range(0, PIECE, P):
                diff = psum_res.tile([P, PACK, P], F32, name="diff", tag="res")
                for t in range(PACK):
                    nc.tensor.matmul(
                        diff[:, t, :], lhsT=rows[:, t, r0 + m0 : r0 + m0 + P], rhs=eye[:],
                        start=True, stop=False, is_transpose=True,
                    )
                    nc.tensor.matmul(
                        diff[:, t, :], lhsT=neg[:, t, m0 : m0 + P], rhs=eye[:],
                        start=False, stop=True, is_transpose=True,
                    )
                pairs = turns.tile([P, 2, P, 2], BF16, name="pairs", tag="pairs")
                nc.scalar.copy(out=pairs[:], in_=diff[:].rearrange("n (u e) p -> n u p e", e=2))
                turned.append(pairs)
            words = psum_res.tile([P, 2, 2, P], F32, name="words", tag="res")
            for i, pairs in enumerate(turned):
                as_words = pairs[:].rearrange("n u p e -> n (u p e)").bitcast(F32)
                for u in range(2):
                    nc.tensor.transpose(words[:, i, u, :], as_words[:, u * P : (u + 1) * P], eye[:])
            left = staged()
            nc.scalar.copy(
                out=left[:].rearrange("p w t -> p (w t)").bitcast(F32).rearrange("p (i n u) -> p i n u", i=2, u=2),
                in_=words[:].rearrange("p i u n -> p i n u"),
            )
            quantise(wr[a][s], 0, left)

        def list_half(sb, h):
            return sb[:, h * HALF // LIST_ROWS : (h + 1) * HALF // LIST_ROWS]

        def gather(dst, plane, h):
            nc.vector.tensor_tensor(dst, plane[:].indirect(list_half(offs_sb, h)), wgt_sb[h][:], ALU.mult)

        def finish(h, m, y):
            s, m0 = divmod(m * P, PIECE)
            acc = psum_acc.tile([P, HALF], F32, name="acc", tag="acc")
            terms = [(wq[0], xq[0][h]), (wr[0], xq[0][h]), (wq[1], xq[1][h]), (wr[1], xq[1][h]), (wxq, cq[h])]
            for n, (lhs, rhs) in enumerate(terms):
                mm(acc[:], lhs[s], m0, rhs, n == 0, n == len(terms) - 1)
            nc.scalar.activation(out=y[:], in_=acc[:], func=ACT.Identity, bias=bias[:, m : m + 1], scale=1.0)
            nc.vector.tensor_tensor(pages[m][:].indirect(list_half(offs2_sb, h)), y[:], wgo_sb[h][:], ALU.mult)

        def ring_y():
            return ybuf.tile([P, HALF], F32, name="y", tag="y")

        picked0 = [keep.tile([P, PACK, HALF], F32, name="picked0", tag="picked0_%d" % h, align_bytes=64) for h in range(2)]
        early = keep.tile([P, PACK, HALF], F32, name="early")
        planes = []

        def gather_first_pass(t, plane):
            for h in range(2):
                gather(picked0[h][:, t, :], plane, h)

        def gather_early(t):
            planes.append(load_plane(1, t))
            gather(early[:, t, :], planes[t], 0)

        wt0 = load_rows(wt[0:K_PASS, :], ring_rows())
        nc.sync.dma_start(out=wgt_sb[0][:], in_=wgt[:, 0:HALF])
        plane = load_plane(0, 0)
        nc.sync.dma_start(out=wgt_sb[1][:], in_=wgt[:, HALF:J])
        wt1 = load_rows(wt[K_PASS:K, :], ring_rows())
        stationary(wq[0], wt0)
        for s in range(2):
            second_tier_on_vector(0, s, wt0, s * PIECE, staged())
        gather_first_pass(0, plane)
        for s in range(2):
            round_and_quantise(wq[1][s], 0, wt1, s * PIECE, named_stage("page%d" % (2 + s), PIECE))
            clear_page(2 + s, nc.gpsimd, HALF)
        for s in range(2):
            second_tier(1, s, wt1, s * PIECE)
        for t in range(1, PACK):
            gather_first_pass(t, load_plane(0, t))
        nc.sync.dma_start(out=bias_rows[0:N_TILES, :], in_=b.rearrange("(m p) -> m p", p=P))
        bias_turned = psum_res.tile([P, P], F32, name="bias_turned", tag="res")
        nc.tensor.transpose(bias_turned[:], bias_rows[:], eye[:])
        nc.scalar.copy(out=bias[:], in_=bias_turned[:, 0:N_TILES])
        round_and_quantise(xq[0][0], 0, picked0[0], 0, named_stage("wide", HALF))

        gather_early(0)
        gather_early(1)
        wx_rows = load_rows(wx, ring_rows())
        stationary(wxq, wx_rows)
        gather_early(2)
        gather_early(3)
        c_early = load_rows(c[:, 0:HALF], ring_rows())
        nc.sync.dma_start(out=wgo_sb[0][:], in_=wgo[:, 0:HALF])
        nc.sync.dma_start(offs2_sb[:], offs2)
        c_late = load_rows(c[:, HALF:J], keep.tile([P, PACK, HALF], F32, name="c_late", tag="c_late"))
        nc.sync.dma_start(out=wgo_sb[1][:], in_=wgo[:, HALF:J])

        late_row = keep.tile([P, PACK * HALF], F32, name="late_row", tag="wgt0", align_bytes=64)
        late = late_row[:].rearrange("p (t w) -> p t w", t=PACK)

        def borrowed(t):
            return late_row[:, t * HALF : (t + 1) * HALF].bitcast(BF16).rearrange("p (w t) -> p w t", t=PACK)

        moving(xq[1][0], early, [staged(), borrowed(3)])
        moving(cq[0], c_early, [named_stage("hold", PIECE), borrowed(2)])
        for t in (0, 1, 3, 2):
            gather(late_row[:, t * HALF : (t + 1) * HALF], planes[t], 1)
        finish(0, 0, ring_y())
        finish(0, 1, ring_y())
        round_and_quantise(xq[0][1], 0, picked0[1], 0, named_stage("hold", HALF))
        round_and_quantise(xq[1][1], 0, late, 0, named_stage("wide", HALF))
        round_and_quantise(cq[1], 0, c_late, 0, named_stage("hold", HALF))
        finish(0, 2, keep.tile([P, HALF], F32, name="y_after_late", tag="wgt0", align_bytes=64))
        finish(0, 3, keep.tile([P, HALF], F32, name="y_after_c", tag="c_late"))
        for m in range(N_TILES):
            finish(1, m, ring_y())
            nc.sync.dma_start(out=out[m * P : (m + 1) * P, :], in_=pages[m][:])
